import numpy as np
import ml_dtypes


def mxq(x, axis, fmt="e4m3"):
    dtype, down = {"e4m3": (ml_dtypes.float8_e4m3fn, 7), "e5m2": (ml_dtypes.float8_e5m2, 14)}[fmt]
    v = np.moveaxis(np.asarray(x, np.float32).astype(ml_dtypes.bfloat16).astype(np.float64), axis, -1)
    blocks = v.reshape(v.shape[:-1] + (-1, 32))
    amax = np.abs(blocks).max(-1, keepdims=True)
    byte = np.maximum(np.where(amax > 0, np.frexp(amax)[1] - 1 + 127, 0) - down, 1)
    scale = np.exp2(byte - 127.0)
    codes = (blocks / scale).astype(np.float32).astype(dtype).astype(np.float64)
    return np.moveaxis((codes * scale).reshape(v.shape), -1, axis)


WIDE = False


def mx_kscale(k):
    if not WIDE:
        return np.ones(k)
    levels = np.array([10, -10, 5, -5, 0])
    if k % 512:
        return np.exp2(np.random.permutation(np.resize(levels, k // 32))).repeat(32)
    a = np.empty((k // 512, 16))
    for p in range(k // 512):
        a[p, :8] = np.random.permutation(np.resize(levels, 8))
        for g in range(8):
            far = levels[np.abs(levels - a[p, g]) >= 10]
            a[p, g + 8] = far[np.random.randint(len(far))]
    return np.exp2(a.ravel()).repeat(32)


def f64(x):
    return np.asarray(x).astype(np.float64)


def striped(idx):
    return np.tile(idx.reshape(-1, 16).T, (8, 1)).astype(np.uint16)


def unstriped(offs):
    return offs[:16].T.reshape(-1).astype(np.int64)


def gelu(v):
    return 0.5 * v * (1.0 + np.tanh(np.sqrt(2.0 / np.pi) * (v + 0.044715 * v**3)))


K, T, S, H, N = 512, 2048, 512, 512, 128


def setup_inputs():
    n = np.random.standard_normal
    s = mx_kscale(K)[:, None]
    u = mx_kscale(H)
    return {
        "xT": (n((K, T)) * s).astype(np.float32),
        "w1": (n((K, H)) / np.sqrt(K) / s * u).astype(np.float32),
        "w2": (n((H, N)) / np.sqrt(H) / u[:, None]).astype(np.float32),
        "pe": (0.5 * n((H, T)) * u[:, None]).astype(np.float32),
        "offs": striped(np.random.permutation(T)[:S]),
    }


def reference(xT, w1, w2, pe, offs):
    xq = mxq(f64(xT)[:, unstriped(offs)], 0, "e4m3")
    g = f64(pe)[:, unstriped(offs)]
    h = gelu((mxq(f64(w1), 0, "e4m3").T @ xq) + g)
    return mxq(f64(w2), 0, "e4m3").T @ mxq(h, 0, "e4m3")

@@ -1,0 +1,120 @@
+from contextlib import ExitStack
+
+import concourse.mybir as mybir
+
+K, T, S, H, N = 512, 2048, 512, 512, 128
+FLOPS = 2 * K * H * S + 2 * H * N * S
+
+F32 = mybir.dt.float32
+BF16 = mybir.dt.bfloat16
+U32 = mybir.dt.uint32
+U16 = mybir.dt.uint16
+U8 = mybir.dt.uint8
+FP8X4 = mybir.dt.float8_e4m3fn_x4
+GELU = mybir.ActivationFunctionType.Gelu_apprx_tanh
+ADD = mybir.AluOpType.add
+
+P = 128
+PACK = 4
+SLICES = [128,128,128,128]
+
+
+def quantise(nc, pool, grouped, name):
+    width = grouped.shape[1]
+    codes = pool.tile([P, width], U32, name=name + "_codes", align_bytes=64)
+    scales = pool.tile([P, width], U8, name=name + "_scales", align_bytes=64)
+    nc.vector.quantize_mx(out=codes[:].bitcast(FP8X4), scales=scales[:], in_=grouped[:].rearrange("p w j -> p (w j)"))
+    return codes, scales
+
+
+def tile_picked_posadd_gelu_l_kernel(tc, xT, w1, w2, pe, offs, out):
+    nc = tc.nc
+    with ExitStack() as ctx:
+        pool = ctx.enter_context(tc.tile_pool(name="pool", bufs=1))
+        psum = ctx.enter_context(tc.psum_pool(name="psum", bufs=1))
+
+        offsets = pool.tile([P, S // 16], U16, name="offsets")
+        w1_raw = pool.tile([P, PACK, H], F32, name="w1_raw")
+        w2_raw = pool.tile([P, PACK, N], F32, name="w2_raw")
+        x_rows = [pool.tile([P, T], F32, name="x_rows%d" % j) for j in range(PACK)]
+        pe_rows = [pool.tile([P, T], F32, name="pe_rows%d" % t) for t in range(PACK)]
+        x_view = xT.rearrange("(p j) c -> p j c", j=PACK)
+        pe_view = pe.rearrange("(p t) c -> p t c", t=PACK)
+
+        nc.sync.dma_start(out=w1_raw[:], in_=w1.rearrange("(p j) c -> p j c", j=PACK))
+        nc.sync.dma_start(offsets[:], offs)
+        nc.sync.dma_start(out=w2_raw[:], in_=w2.rearrange("(p j) c -> p j c", j=PACK))
+        for j in range(PACK):
+            nc.sync.dma_start(out=x_rows[j][:], in_=x_view[:, j, :])
+        for t in range(PACK):
+            nc.sync.dma_start(out=pe_rows[t][:], in_=pe_view[:, t, :])
+
+        w1_grouped = pool.tile([P, H, PACK], BF16, name="w1_grouped", align_bytes=64)
+        nc.scalar.copy(
+            out=w1_grouped[:].rearrange("p (t m) j -> p m j t", t=PACK),
+            in_=w1_raw[:].rearrange("p j (m t) -> p m j t", t=PACK),
+        )
+        w1_codes, w1_scales = quantise(nc, pool, w1_grouped, "w1")
+
+        w2_grouped = pool.tile([P, N, PACK], BF16, name="w2_grouped", align_bytes=64)
+        nc.scalar.copy(out=w2_grouped[:], in_=w2_raw[:].rearrange("p j c -> p c j"))
+        w2_codes, w2_scales = quantise(nc, pool, w2_grouped, "w2")
+
+        x_grouped = pool.tile([P, S, PACK], BF16, name="x_grouped", align_bytes=64)
+        for j in range(PACK):
+            nc.vector.tensor_copy(x_grouped[:, :, j], x_rows[j][:].indirect(offsets[:]))
+        x_codes, x_scales = quantise(nc, pool, x_grouped, "x")
+
+        product = []
+        for t in range(PACK):
+            bank = psum.tile([P, S], F32, name="h_bank%d" % t)
+            nc.tensor.matmul_mx(
+                out=bank[:],
+                lhsT=w1_codes[:, t * P : (t + 1) * P].bitcast(FP8X4),
+                lhsT_scale=w1_scales[:, t * P : (t + 1) * P],
+                rhs=x_codes[:].bitcast(FP8X4),
+                rhs_scale=x_scales[:],
+                start=True,
+                stop=True,
+            )
+            moved = pool.tile([P, S], F32, name="product%d" % t)
+            nc.scalar.copy(out=moved[:], in_=bank[:])
+            product.append(moved)
+
+        starts = [sum(SLICES[:s]) for s in range(len(SLICES))]
+        h_grouped = [pool.tile([P, n, PACK], BF16, name="h_grouped%d" % s, align_bytes=64) for s, n in enumerate(SLICES)]
+
+        early = pool.tile([P, 2, S], F32, name="early")
+        for t in range(2):
+            nc.vector.tensor_tensor(early[:, t, :], pe_rows[t][:].indirect(offsets[:]), product[t][:], ADD)
+        for s, n in enumerate(SLICES):
+            cols = slice(starts[s], starts[s] + n)
+            nc.scalar.activation(h_grouped[s][:, :, 0:2], early[:, :, cols].rearrange("p t n -> p n t"), GELU)
+
+        late = [pool.tile([P, 2, n], F32, name="late%d" % s) for s, n in enumerate(SLICES)]
+        for t in range(2, PACK):
+            for s, n in enumerate(SLICES):
+                cols = slice(starts[s], starts[s] + n)
+                entries = offsets[:, starts[s] // 16 : (starts[s] + n) // 16]
+                nc.vector.tensor_tensor(late[s][:, t - 2, :], pe_rows[t][:].indirect(entries), product[t][:, cols], ADD)
+        for s, n in enumerate(SLICES):
+            nc.scalar.activation(h_grouped[s][:, :, 2:4], late[s][:].rearrange("p t n -> p n t"), GELU)
+        for s, n in enumerate(SLICES):
+            cols = slice(starts[s], starts[s] + n)
+            h_codes, h_scales = quantise(nc, pool, h_grouped[s], "h%d" % s)
+            bank = psum.tile([P, n], F32, name="out_bank%d" % s)
+            nc.tensor.matmul_mx(
+                out=bank[:],
+                lhsT=w2_codes[:].bitcast(FP8X4),
+                lhsT_scale=w2_scales[:],
+                rhs=h_codes[:].bitcast(FP8X4),
+                rhs_scale=h_scales[:],
+                start=True,
+                stop=True,
+            )
+            result = pool.tile([P, n], F32, name="result%d" % s)
+            if s == len(SLICES) - 1:
+                nc.vector.tensor_copy(out=result[:], in_=bank[:])
+            else:
+                nc.scalar.copy(out=result[:], in_=bank[:])
+            nc.sync.dma_start(out=out[:, cols], in_=result[:])

@@ -16,7 +16,7 @@ ADD = mybir.AluOpType.add
 
 P = 128
 PACK = 4
-SLICES = [128,128,128,128]
+SLICES = [64,128,128,128,64]
 
 
 def quantise(nc, pool, grouped, name):
@@ -43,11 +43,16 @@ def tile_picked_posadd_gelu_l_kernel(tc, xT, w1, w2, pe, offs, out):
 
         nc.sync.dma_start(out=w1_raw[:], in_=w1.rearrange("(p j) c -> p j c", j=PACK))
         nc.sync.dma_start(offsets[:], offs)
-        nc.sync.dma_start(out=w2_raw[:], in_=w2.rearrange("(p j) c -> p j c", j=PACK))
         for j in range(PACK):
             nc.sync.dma_start(out=x_rows[j][:], in_=x_view[:, j, :])
+        nc.sync.dma_start(out=w2_raw[:], in_=w2.rearrange("(p j) c -> p j c", j=PACK))
         for t in range(PACK):
             nc.sync.dma_start(out=pe_rows[t][:], in_=pe_view[:, t, :])
+
+        warm_in = pool.tile([P, 1], F32, name="warm_in")
+        warm_out = pool.tile([P, 1], F32, name="warm_out")
+        nc.vector.memset(warm_in[:], 0.0)
+        nc.scalar.activation(warm_out[:], warm_in[:], GELU)
 
         w1_grouped = pool.tile([P, H, PACK], BF16, name="w1_grouped", align_bytes=64)
         nc.scalar.copy(
@@ -58,16 +63,16 @@ def tile_picked_posadd_gelu_l_kernel(tc, xT, w1, w2, pe, offs, out):
 
         w2_grouped = pool.tile([P, N, PACK], BF16, name="w2_grouped", align_bytes=64)
         nc.scalar.copy(out=w2_grouped[:], in_=w2_raw[:].rearrange("p j c -> p c j"))
-        w2_codes, w2_scales = quantise(nc, pool, w2_grouped, "w2")
 
         x_grouped = pool.tile([P, S, PACK], BF16, name="x_grouped", align_bytes=64)
         for j in range(PACK):
             nc.vector.tensor_copy(x_grouped[:, :, j], x_rows[j][:].indirect(offsets[:]))
         x_codes, x_scales = quantise(nc, pool, x_grouped, "x")
+        w2_codes, w2_scales = quantise(nc, pool, w2_grouped, "w2")
 
         product = []
         for t in range(PACK):
-            bank = psum.tile([P, S], F32, name="h_bank%d" % t)
+            bank = psum.tile([P, S], F32, name="bank%d" % t)
             nc.tensor.matmul_mx(
                 out=bank[:],
                 lhsT=w1_codes[:, t * P : (t + 1) * P].bitcast(FP8X4),
@@ -102,7 +107,7 @@ def tile_picked_posadd_gelu_l_kernel(tc, xT, w1, w2, pe, offs, out):
         for s, n in enumerate(SLICES):
             cols = slice(starts[s], starts[s] + n)
             h_codes, h_scales = quantise(nc, pool, h_grouped[s], "h%d" % s)
-            bank = psum.tile([P, n], F32, name="out_bank%d" % s)
+            bank = psum.tile([P, n], F32, name="bank%d" % ((s + PACK) % 8))
             nc.tensor.matmul_mx(
                 out=bank[:],
                 lhsT=w2_codes[:].bitcast(FP8X4),

@@ -41,7 +41,7 @@ def tile_picked_posadd_gelu_l_kernel(tc, xT, w1, w2, pe, offs, out):
         x_view = xT.rearrange("(p j) c -> p j c", j=PACK)
         pe_view = pe.rearrange("(p t) c -> p t c", t=PACK)
 
-        nc.sync.dma_start(out=w1_raw[:], in_=w1.rearrange("(p j) c -> p j c", j=PACK))
+        nc.scalar.dma_start(out=w1_raw[:], in_=w1.rearrange("(p j) c -> p j c", j=PACK))
         nc.sync.dma_start(offsets[:], offs)
         for j in range(PACK):
             nc.sync.dma_start(out=x_rows[j][:], in_=x_view[:, j, :])
@@ -120,6 +120,7 @@ def tile_picked_posadd_gelu_l_kernel(tc, xT, w1, w2, pe, offs, out):
             result = pool.tile([P, n], F32, name="result%d" % s)
             if s == len(SLICES) - 1:
                 nc.vector.tensor_copy(out=result[:], in_=bank[:])
+                nc.scalar.dma_start(out=out[:, cols], in_=result[:])
             else:
                 nc.scalar.copy(out=result[:], in_=bank[:])
-            nc.sync.dma_start(out=out[:, cols], in_=result[:])
+                nc.sync.dma_start(out=out[:, cols], in_=result[:])

@@ -45,9 +45,9 @@ def tile_picked_posadd_gelu_l_kernel(tc, xT, w1, w2, pe, offs, out):
         nc.sync.dma_start(offsets[:], offs)
         for j in range(PACK):
             nc.sync.dma_start(out=x_rows[j][:], in_=x_view[:, j, :])
-        nc.sync.dma_start(out=w2_raw[:], in_=w2.rearrange("(p j) c -> p j c", j=PACK))
         for t in range(PACK):
             nc.sync.dma_start(out=pe_rows[t][:], in_=pe_view[:, t, :])
+        nc.sync.dma_start(out=w2_raw[:], in_=w2.rearrange("(p j) c -> p j c", j=PACK))
 
         warm_in = pool.tile([P, 1], F32, name="warm_in")
         warm_out = pool.tile([P, 1], F32, name="warm_out")
@@ -61,14 +61,10 @@ def tile_picked_posadd_gelu_l_kernel(tc, xT, w1, w2, pe, offs, out):
         )
         w1_codes, w1_scales = quantise(nc, pool, w1_grouped, "w1")
 
-        w2_grouped = pool.tile([P, N, PACK], BF16, name="w2_grouped", align_bytes=64)
-        nc.scalar.copy(out=w2_grouped[:], in_=w2_raw[:].rearrange("p j c -> p c j"))
-
         x_grouped = pool.tile([P, S, PACK], BF16, name="x_grouped", align_bytes=64)
         for j in range(PACK):
             nc.vector.tensor_copy(x_grouped[:, :, j], x_rows[j][:].indirect(offsets[:]))
         x_codes, x_scales = quantise(nc, pool, x_grouped, "x")
-        w2_codes, w2_scales = quantise(nc, pool, w2_grouped, "w2")
 
         product = []
         for t in range(PACK):
@@ -102,6 +98,12 @@ def tile_picked_posadd_gelu_l_kernel(tc, xT, w1, w2, pe, offs, out):
                 cols = slice(starts[s], starts[s] + n)
                 entries = offsets[:, starts[s] // 16 : (starts[s] + n) // 16]
                 nc.vector.tensor_tensor(late[s][:, t - 2, :], pe_rows[t][:].indirect(entries), product[t][:, cols], ADD)
+        w2_grouped = pool.tile([P, N, PACK], BF16, name="w2_grouped", align_bytes=64)
+        nc.vector.tensor_copy(
+            out=w2_grouped[:].rearrange("p (c i) j -> p c j i", i=PACK),
+            in_=w2_raw[:].rearrange("p j (c i) -> p c j i", i=PACK),
+        )
+        w2_codes, w2_scales = quantise(nc, pool, w2_grouped, "w2")
         for s, n in enumerate(SLICES):
             nc.scalar.activation(h_grouped[s][:, :, 2:4], late[s][:].rearrange("p t n -> p n t"), GELU)
         for s, n in enumerate(SLICES):

@@ -49,11 +49,6 @@ def tile_picked_posadd_gelu_l_kernel(tc, xT, w1, w2, pe, offs, out):
             nc.sync.dma_start(out=pe_rows[t][:], in_=pe_view[:, t, :])
         nc.sync.dma_start(out=w2_raw[:], in_=w2.rearrange("(p j) c -> p j c", j=PACK))
 
-        warm_in = pool.tile([P, 1], F32, name="warm_in")
-        warm_out = pool.tile([P, 1], F32, name="warm_out")
-        nc.vector.memset(warm_in[:], 0.0)
-        nc.scalar.activation(warm_out[:], warm_in[:], GELU)
-
         w1_grouped = pool.tile([P, H, PACK], BF16, name="w1_grouped", align_bytes=64)
         nc.scalar.copy(
             out=w1_grouped[:].rearrange("p (t m) j -> p m j t", t=PACK),
@@ -65,8 +60,11 @@ def tile_picked_posadd_gelu_l_kernel(tc, xT, w1, w2, pe, offs, out):
         for j in range(PACK):
             nc.vector.tensor_copy(x_grouped[:, :, j], x_rows[j][:].indirect(offsets[:]))
         x_codes, x_scales = quantise(nc, pool, x_grouped, "x")
+        pe_picked = pool.tile([P, S], F32, name="pe_picked")
+        nc.vector.tensor_copy(pe_picked[:], pe_rows[0][:].indirect(offsets[:]))
+        early = pool.tile([P, 2, S], F32, name="early")
 
-        product = []
+        product = {}
         for t in range(PACK):
             bank = psum.tile([P, S], F32, name="bank%d" % t)
             nc.tensor.matmul_mx(
@@ -78,16 +76,16 @@ def tile_picked_posadd_gelu_l_kernel(tc, xT, w1, w2, pe, offs, out):
                 start=True,
                 stop=True,
             )
-            moved = pool.tile([P, S], F32, name="product%d" % t)
-            nc.scalar.copy(out=moved[:], in_=bank[:])
-            product.append(moved)
+            if t == 0:
+                nc.vector.tensor_tensor(early[:, 0, :], bank[:], pe_picked[:], ADD)
+            else:
+                product[t] = pool.tile([P, S], F32, name="product%d" % t)
+                nc.scalar.copy(out=product[t][:], in_=bank[:])
 
         starts = [sum(SLICES[:s]) for s in range(len(SLICES))]
         h_grouped = [pool.tile([P, n, PACK], BF16, name="h_grouped%d" % s, align_bytes=64) for s, n in enumerate(SLICES)]
 
-        early = pool.tile([P, 2, S], F32, name="early")
-        for t in range(2):
-            nc.vector.tensor_tensor(early[:, t, :], pe_rows[t][:].indirect(offsets[:]), product[t][:], ADD)
+        nc.vector.tensor_tensor(early[:, 1, :], pe_rows[1][:].indirect(offsets[:]), product[1][:], ADD)
         for s, n in enumerate(SLICES):
             cols = slice(starts[s], starts[s] + n)
             nc.scalar.activation(h_grouped[s][:, :, 0:2], early[:, :, cols].rearrange("p t n -> p n t"), GELU)

@@ -42,9 +42,10 @@ def tile_picked_posadd_gelu_l_kernel(tc, xT, w1, w2, pe, offs, out):
         pe_view = pe.rearrange("(p t) c -> p t c", t=PACK)
 
         nc.scalar.dma_start(out=w1_raw[:], in_=w1.rearrange("(p j) c -> p j c", j=PACK))
-        nc.sync.dma_start(offsets[:], offs)
         for j in range(PACK):
             nc.sync.dma_start(out=x_rows[j][:], in_=x_view[:, j, :])
+            if j == 0:
+                nc.sync.dma_start(offsets[:], offs)
         for t in range(PACK):
             nc.sync.dma_start(out=pe_rows[t][:], in_=pe_view[:, t, :])
         nc.sync.dma_start(out=w2_raw[:], in_=w2.rearrange("(p j) c -> p j c", j=PACK))

@@ -16,7 +16,8 @@ ADD = mybir.AluOpType.add
 
 P = 128
 PACK = 4
-SLICES = [64,128,128,128,64]
+SLICES = [64, 128, 128, 128, 64]
+GATHERS = [64, 128, 160, 160]
 
 
 def quantise(nc, pool, grouped, name):
@@ -91,12 +92,13 @@ def tile_picked_posadd_gelu_l_kernel(tc, xT, w1, w2, pe, offs, out):
             cols = slice(starts[s], starts[s] + n)
             nc.scalar.activation(h_grouped[s][:, :, 0:2], early[:, :, cols].rearrange("p t n -> p n t"), GELU)
 
-        late = [pool.tile([P, 2, n], F32, name="late%d" % s) for s, n in enumerate(SLICES)]
-        for t in range(2, PACK):
-            for s, n in enumerate(SLICES):
-                cols = slice(starts[s], starts[s] + n)
-                entries = offsets[:, starts[s] // 16 : (starts[s] + n) // 16]
-                nc.vector.tensor_tensor(late[s][:, t - 2, :], pe_rows[t][:].indirect(entries), product[t][:, cols], ADD)
+        late = pool.tile([P, 2 * S], F32, name="late")
+        nc.vector.tensor_tensor(late[:, :S], pe_rows[2][:].indirect(offsets[:]), product[2][:], ADD)
+        for s, n in enumerate(GATHERS):
+            first = sum(GATHERS[:s])
+            entries = offsets[:, first // 16 : (first + n) // 16]
+            nc.vector.tensor_tensor(late[:, S + first : S + first + n], pe_rows[3][:].indirect(entries), product[3][:, first : first + n], ADD)
+        late_planes = late[:].rearrange("p (t n) -> p n t", t=2)
         w2_grouped = pool.tile([P, N, PACK], BF16, name="w2_grouped", align_bytes=64)
         nc.vector.tensor_copy(
             out=w2_grouped[:].rearrange("p (c i) j -> p c j i", i=PACK),
@@ -104,7 +106,7 @@ def tile_picked_posadd_gelu_l_kernel(tc, xT, w1, w2, pe, offs, out):
         )
         w2_codes, w2_scales = quantise(nc, pool, w2_grouped, "w2")
         for s, n in enumerate(SLICES):
-            nc.scalar.activation(h_grouped[s][:, :, 2:4], late[s][:].rearrange("p t n -> p n t"), GELU)
+            nc.scalar.activation(h_grouped[s][:, :, 2:4], late_planes[:, starts[s] : starts[s] + n, :], GELU)
         for s, n in enumerate(SLICES):
             cols = slice(starts[s], starts[s] + n)
             h_codes, h_scales = quantise(nc, pool, h_grouped[s], "h%d" % s)

@@ -16,6 +16,7 @@ ADD = mybir.AluOpType.add
 
 P = 128
 PACK = 4
+HALF = S // 2
 SLICES = [64, 128, 128, 128, 64]
 GATHERS = [64, 128, 160, 160]
 
@@ -37,17 +38,21 @@ def tile_picked_posadd_gelu_l_kernel(tc, xT, w1, w2, pe, offs, out):
         offsets = pool.tile([P, S // 16], U16, name="offsets")
         w1_raw = pool.tile([P, PACK, H], F32, name="w1_raw")
         w2_raw = pool.tile([P, PACK, N], F32, name="w2_raw")
-        x_rows = [pool.tile([P, T], F32, name="x_rows%d" % j) for j in range(PACK)]
-        pe_rows = [pool.tile([P, T], F32, name="pe_rows%d" % t) for t in range(PACK)]
-        x_view = xT.rearrange("(p j) c -> p j c", j=PACK)
+        x_pairs = [pool.tile([P, 2 * T], F32, name="x_pair%d" % u) for u in range(2)]
+        pe_pair = pool.tile([P, 2 * T], F32, name="pe_pair")
+        pe_rows = {t: pool.tile([P, T], F32, name="pe_rows%d" % t) for t in (2, 3)}
+        x_view = xT.rearrange("(p u e) c -> p u (e c)", u=2, e=2)
+        pe_pair_view = pe.rearrange("(p u e) c -> p u (e c)", u=2, e=2)
         pe_view = pe.rearrange("(p t) c -> p t c", t=PACK)
 
+        warm = pool.tile([P, 1], F32, name="warm")
         nc.scalar.dma_start(out=w1_raw[:], in_=w1.rearrange("(p j) c -> p j c", j=PACK))
-        for j in range(PACK):
-            nc.sync.dma_start(out=x_rows[j][:], in_=x_view[:, j, :])
-            if j == 0:
-                nc.sync.dma_start(offsets[:], offs)
-        for t in range(PACK):
+        nc.scalar.activation(warm[:], w1_raw[:, 0, 0:1], GELU)
+        nc.sync.dma_start(out=x_pairs[0][:], in_=x_view[:, 0, :])
+        nc.sync.dma_start(offsets[:], offs)
+        nc.sync.dma_start(out=x_pairs[1][:], in_=x_view[:, 1, :])
+        nc.sync.dma_start(out=pe_pair[:], in_=pe_pair_view[:, 0, :])
+        for t in (2, 3):
             nc.sync.dma_start(out=pe_rows[t][:], in_=pe_view[:, t, :])
         nc.sync.dma_start(out=w2_raw[:], in_=w2.rearrange("(p j) c -> p j c", j=PACK))
 
@@ -58,46 +63,65 @@ def tile_picked_posadd_gelu_l_kernel(tc, xT, w1, w2, pe, offs, out):
         )
         w1_codes, w1_scales = quantise(nc, pool, w1_grouped, "w1")
 
-        x_grouped = pool.tile([P, S, PACK], BF16, name="x_grouped", align_bytes=64)
-        for j in range(PACK):
-            nc.vector.tensor_copy(x_grouped[:, :, j], x_rows[j][:].indirect(offsets[:]))
-        x_codes, x_scales = quantise(nc, pool, x_grouped, "x")
-        pe_picked = pool.tile([P, S], F32, name="pe_picked")
-        nc.vector.tensor_copy(pe_picked[:], pe_rows[0][:].indirect(offsets[:]))
-        early = pool.tile([P, 2, S], F32, name="early")
-
-        product = {}
-        for t in range(PACK):
-            bank = psum.tile([P, S], F32, name="bank%d" % t)
+        def first_product(dest, t, codes, scales):
             nc.tensor.matmul_mx(
-                out=bank[:],
+                out=dest,
                 lhsT=w1_codes[:, t * P : (t + 1) * P].bitcast(FP8X4),
                 lhsT_scale=w1_scales[:, t * P : (t + 1) * P],
-                rhs=x_codes[:].bitcast(FP8X4),
-                rhs_scale=x_scales[:],
+                rhs=codes[:].bitcast(FP8X4),
+                rhs_scale=scales[:],
                 start=True,
                 stop=True,
             )
-            if t == 0:
-                nc.vector.tensor_tensor(early[:, 0, :], bank[:], pe_picked[:], ADD)
-            else:
-                product[t] = pool.tile([P, S], F32, name="product%d" % t)
-                nc.scalar.copy(out=product[t][:], in_=bank[:])
+
+        x_grouped = [pool.tile([P, HALF, PACK], BF16, name="x_grouped%d" % a, align_bytes=64) for a in range(2)]
+        lists = [offsets[:, a * HALF // 16 : (a + 1) * HALF // 16] for a in range(2)]
+        for a in range(2):
+            for j in range(2):
+                nc.vector.tensor_copy(x_grouped[a][:, :, j], x_pairs[0][:, j * T : (j + 1) * T].indirect(lists[a]))
+        x_late = [pool.tile([P, 2, HALF], F32, name="x_late%d" % a) for a in range(2)]
+        for a in range(2):
+            for j in range(2):
+                nc.vector.tensor_copy(x_late[a][:, j, :], x_pairs[1][:, j * T : (j + 1) * T].indirect(lists[a]))
+            nc.scalar.copy(out=x_grouped[a][:, :, 2:4], in_=x_late[a][:].rearrange("p j n -> p n j"))
+
+        early = pool.tile([P, 2, S], F32, name="early")
+        product0 = pool.tile([P, S], F32, name="product0")
+        product23 = pool.tile([P, 2, S], F32, name="product23")
+        banks1 = []
+        for a in range(2):
+            cols = slice(a * HALF, (a + 1) * HALF)
+            x_codes, x_scales = quantise(nc, pool, x_grouped[a], "x%d" % a)
+            bank0 = psum.tile([P, HALF], F32, name="bank%d" % (3 * a))
+            bank1 = psum.tile([P, HALF], F32, name="bank%d" % (3 * a + 1))
+            bank23 = psum.tile([P, 2, HALF], F32, name="bank%d" % (3 * a + 2))
+            first_product(bank0[:], 0, x_codes, x_scales)
+            first_product(bank1[:], 1, x_codes, x_scales)
+            first_product(bank23[:, 0, :], 2, x_codes, x_scales)
+            first_product(bank23[:, 1, :], 3, x_codes, x_scales)
+            nc.scalar.copy(out=product0[:, cols], in_=bank0[:])
+            nc.scalar.copy(out=product23[:, :, cols], in_=bank23[:])
+            banks1.append(bank1)
+        pe_picked = pool.tile([P, S], F32, name="pe_picked")
+        for a in range(2):
+            cols = slice(a * HALF, (a + 1) * HALF)
+            nc.vector.tensor_copy(pe_picked[:, cols], pe_pair[:, T:].indirect(lists[a]))
+            nc.vector.tensor_tensor(early[:, 0, cols], pe_pair[:].indirect(lists[a]), product0[:, cols], ADD)
+            nc.vector.tensor_tensor(early[:, 1, cols], banks1[a][:], pe_picked[:, cols], ADD)
 
         starts = [sum(SLICES[:s]) for s in range(len(SLICES))]
         h_grouped = [pool.tile([P, n, PACK], BF16, name="h_grouped%d" % s, align_bytes=64) for s, n in enumerate(SLICES)]
 
-        nc.vector.tensor_tensor(early[:, 1, :], pe_rows[1][:].indirect(offsets[:]), product[1][:], ADD)
         for s, n in enumerate(SLICES):
             cols = slice(starts[s], starts[s] + n)
             nc.scalar.activation(h_grouped[s][:, :, 0:2], early[:, :, cols].rearrange("p t n -> p n t"), GELU)
 
         late = pool.tile([P, 2 * S], F32, name="late")
-        nc.vector.tensor_tensor(late[:, :S], pe_rows[2][:].indirect(offsets[:]), product[2][:], ADD)
+        nc.vector.tensor_tensor(late[:, :S], pe_rows[2][:].indirect(offsets[:]), product23[:, 0, :], ADD)
         for s, n in enumerate(GATHERS):
             first = sum(GATHERS[:s])
             entries = offsets[:, first // 16 : (first + n) // 16]
-            nc.vector.tensor_tensor(late[:, S + first : S + first + n], pe_rows[3][:].indirect(entries), product[3][:, first : first + n], ADD)
+            nc.vector.tensor_tensor(late[:, S + first : S + first + n], pe_rows[3][:].indirect(entries), product23[:, 1, first : first + n], ADD)
         late_planes = late[:].rearrange("p (t n) -> p n t", t=2)
         w2_grouped = pool.tile([P, N, PACK], BF16, name="w2_grouped", align_bytes=64)
         nc.vector.tensor_copy(
@@ -110,7 +134,7 @@ def tile_picked_posadd_gelu_l_kernel(tc, xT, w1, w2, pe, offs, out):
         for s, n in enumerate(SLICES):
             cols = slice(starts[s], starts[s] + n)
             h_codes, h_scales = quantise(nc, pool, h_grouped[s], "h%d" % s)
-            bank = psum.tile([P, n], F32, name="bank%d" % ((s + PACK) % 8))
+            bank = psum.tile([P, n], F32, name="bank%d" % ((s + 6) % 8))
             nc.tensor.matmul_mx(
                 out=bank[:],
                 lhsT=w2_codes[:].bitcast(FP8X4),

@@ -18,7 +18,6 @@ P = 128
 PACK = 4
 HALF = S // 2
 SLICES = [64, 128, 128, 128, 64]
-GATHERS = [64, 128, 160, 160]
 
 
 def quantise(nc, pool, grouped, name):
@@ -46,10 +45,10 @@ def tile_picked_posadd_gelu_l_kernel(tc, xT, w1, w2, pe, offs, out):
         pe_view = pe.rearrange("(p t) c -> p t c", t=PACK)
 
         warm = pool.tile([P, 1], F32, name="warm")
-        nc.scalar.dma_start(out=w1_raw[:], in_=w1.rearrange("(p j) c -> p j c", j=PACK))
-        nc.scalar.activation(warm[:], w1_raw[:, 0, 0:1], GELU)
-        nc.sync.dma_start(out=x_pairs[0][:], in_=x_view[:, 0, :])
+        nc.scalar.dma_start(out=x_pairs[0][:], in_=x_view[:, 0, :])
         nc.sync.dma_start(offsets[:], offs)
+        nc.sync.dma_start(out=w1_raw[:], in_=w1.rearrange("(p j) c -> p j c", j=PACK))
+        nc.scalar.activation(warm[:], w1_raw[:, 0, 0:1], GELU)
         nc.sync.dma_start(out=x_pairs[1][:], in_=x_view[:, 1, :])
         nc.sync.dma_start(out=pe_pair[:], in_=pe_pair_view[:, 0, :])
         for t in (2, 3):
@@ -76,14 +75,12 @@ def tile_picked_posadd_gelu_l_kernel(tc, xT, w1, w2, pe, offs, out):
 
         x_grouped = [pool.tile([P, HALF, PACK], BF16, name="x_grouped%d" % a, align_bytes=64) for a in range(2)]
         lists = [offsets[:, a * HALF // 16 : (a + 1) * HALF // 16] for a in range(2)]
-        for a in range(2):
-            for j in range(2):
-                nc.vector.tensor_copy(x_grouped[a][:, :, j], x_pairs[0][:, j * T : (j + 1) * T].indirect(lists[a]))
-        x_late = [pool.tile([P, 2, HALF], F32, name="x_late%d" % a) for a in range(2)]
-        for a in range(2):
-            for j in range(2):
-                nc.vector.tensor_copy(x_late[a][:, j, :], x_pairs[1][:, j * T : (j + 1) * T].indirect(lists[a]))
-            nc.scalar.copy(out=x_grouped[a][:, :, 2:4], in_=x_late[a][:].rearrange("p j n -> p n j"))
+        for u in range(2):
+            for a in range(2):
+                x_picked = pool.tile([P, 2, HALF], F32, name="w1_raw" if u + a == 0 else "x_picked%d%d" % (u, a))
+                for e in range(2):
+                    nc.vector.tensor_copy(x_picked[:, e, :], x_pairs[u][:, e * T : (e + 1) * T].indirect(lists[a]))
+                nc.scalar.copy(out=x_grouped[a][:, :, 2 * u : 2 * u + 2], in_=x_picked[:].rearrange("p e n -> p n e"))
 
         early = pool.tile([P, 2, S], F32, name="early")
         product0 = pool.tile([P, S], F32, name="product0")
@@ -111,26 +108,28 @@ def tile_picked_posadd_gelu_l_kernel(tc, xT, w1, w2, pe, offs, out):
 
         starts = [sum(SLICES[:s]) for s in range(len(SLICES))]
         h_grouped = [pool.tile([P, n, PACK], BF16, name="h_grouped%d" % s, align_bytes=64) for s, n in enumerate(SLICES)]
-
         for s, n in enumerate(SLICES):
             cols = slice(starts[s], starts[s] + n)
             nc.scalar.activation(h_grouped[s][:, :, 0:2], early[:, :, cols].rearrange("p t n -> p n t"), GELU)
 
-        late = pool.tile([P, 2 * S], F32, name="late")
+        late = pool.tile([P, 3 * S], F32, name="late")
         nc.vector.tensor_tensor(late[:, :S], pe_rows[2][:].indirect(offsets[:]), product23[:, 0, :], ADD)
-        for s, n in enumerate(GATHERS):
-            first = sum(GATHERS[:s])
-            entries = offsets[:, first // 16 : (first + n) // 16]
-            nc.vector.tensor_tensor(late[:, S + first : S + first + n], pe_rows[3][:].indirect(entries), product23[:, 1, first : first + n], ADD)
-        late_planes = late[:].rearrange("p (t n) -> p n t", t=2)
+        places = [S + first for first in starts[:-1]] + [S]
         w2_grouped = pool.tile([P, N, PACK], BF16, name="w2_grouped", align_bytes=64)
-        nc.vector.tensor_copy(
-            out=w2_grouped[:].rearrange("p (c i) j -> p c j i", i=PACK),
-            in_=w2_raw[:].rearrange("p j (c i) -> p c j i", i=PACK),
-        )
-        w2_codes, w2_scales = quantise(nc, pool, w2_grouped, "w2")
         for s, n in enumerate(SLICES):
-            nc.scalar.activation(h_grouped[s][:, :, 2:4], late_planes[:, starts[s] : starts[s] + n, :], GELU)
+            first = starts[s]
+            if s == len(SLICES) - 1:
+                nc.vector.tensor_copy(
+                    out=w2_grouped[:].rearrange("p (c i) j -> p c j i", i=PACK),
+                    in_=w2_raw[:].rearrange("p j (c i) -> p c j i", i=PACK),
+                )
+            entries = offsets[:, first // 16 : (first + n) // 16]
+            nc.vector.tensor_tensor(late[:, places[s] : places[s] + n], pe_rows[3][:].indirect(entries), product23[:, 1, first : first + n], ADD)
+            if s == len(SLICES) - 1:
+                w2_codes, w2_scales = quantise(nc, pool, w2_grouped, "w2")
+            apart = places[s] - first
+            planes = late[:, first : first + 2 * apart].rearrange("p (t n) -> p n t", t=2)
+            nc.scalar.activation(h_grouped[s][:, :, 2:4], planes[:, :n, :], GELU)
         for s, n in enumerate(SLICES):
             cols = slice(starts[s], starts[s] + n)
             h_codes, h_scales = quantise(nc, pool, h_grouped[s], "h%d" % s)

@@ -35,11 +35,11 @@ def tile_picked_posadd_gelu_l_kernel(tc, xT, w1, w2, pe, offs, out):
         psum = ctx.enter_context(tc.psum_pool(name="psum", bufs=1))
 
         offsets = pool.tile([P, S // 16], U16, name="offsets")
-        w1_raw = pool.tile([P, PACK, H], F32, name="w1_raw")
-        w2_raw = pool.tile([P, PACK, N], F32, name="w2_raw")
-        x_pairs = [pool.tile([P, 2 * T], F32, name="x_pair%d" % u) for u in range(2)]
-        pe_pair = pool.tile([P, 2 * T], F32, name="pe_pair")
-        pe_rows = {t: pool.tile([P, T], F32, name="pe_rows%d" % t) for t in (2, 3)}
+        w1_raw = pool.tile([P, PACK, H], F32, name="w1_raw", align_bytes=256)
+        w2_raw = pool.tile([P, PACK, N], F32, name="w2_raw", align_bytes=256)
+        x_pairs = [pool.tile([P, 2 * T], F32, name="x_pair%d" % u, align_bytes=256) for u in range(2)]
+        pe_pair = pool.tile([P, 2 * T], F32, name="pe_pair", align_bytes=256)
+        pe_rows = {t: pool.tile([P, T], F32, name="pe_rows%d" % t, align_bytes=256) for t in (2, 3)}
         x_view = xT.rearrange("(p u e) c -> p u (e c)", u=2, e=2)
         pe_pair_view = pe.rearrange("(p u e) c -> p u (e c)", u=2, e=2)
         pe_view = pe.rearrange("(p t) c -> p t c", t=PACK)
@@ -77,7 +77,7 @@ def tile_picked_posadd_gelu_l_kernel(tc, xT, w1, w2, pe, offs, out):
         lists = [offsets[:, a * HALF // 16 : (a + 1) * HALF // 16] for a in range(2)]
         for u in range(2):
             for a in range(2):
-                x_picked = pool.tile([P, 2, HALF], F32, name="w1_raw" if u + a == 0 else "x_picked%d%d" % (u, a))
+                x_picked = pool.tile([P, 2, HALF], F32, name="w1_raw" if u + a == 0 else "x_picked%d%d" % (u, a), align_bytes=256)
                 for e in range(2):
                     nc.vector.tensor_copy(x_picked[:, e, :], x_pairs[u][:, e * T : (e + 1) * T].indirect(lists[a]))
                 nc.scalar.copy(out=x_grouped[a][:, :, 2 * u : 2 * u + 2], in_=x_picked[:].rearrange("p e n -> p n e"))
@@ -143,7 +143,7 @@ def tile_picked_posadd_gelu_l_kernel(tc, xT, w1, w2, pe, offs, out):
                 start=True,
                 stop=True,
             )
-            result = pool.tile([P, n], F32, name="result%d" % s)
+            result = pool.tile([P, n], F32, name="result%d" % s, align_bytes=256)
             if s == len(SLICES) - 1:
                 nc.vector.tensor_copy(out=result[:], in_=bank[:])
                 nc.scalar.dma_start(out=out[:, cols], in_=result[:])

@@ -46,8 +46,8 @@ def tile_picked_posadd_gelu_l_kernel(tc, xT, w1, w2, pe, offs, out):
 
         warm = pool.tile([P, 1], F32, name="warm")
         nc.scalar.dma_start(out=x_pairs[0][:], in_=x_view[:, 0, :])
-        nc.sync.dma_start(offsets[:], offs)
         nc.sync.dma_start(out=w1_raw[:], in_=w1.rearrange("(p j) c -> p j c", j=PACK))
+        nc.sync.dma_start(offsets[:], offs)
         nc.scalar.activation(warm[:], w1_raw[:, 0, 0:1], GELU)
         nc.sync.dma_start(out=x_pairs[1][:], in_=x_view[:, 1, :])
         nc.sync.dma_start(out=pe_pair[:], in_=pe_pair_view[:, 0, :])

@@ -114,6 +114,7 @@ def tile_picked_posadd_gelu_l_kernel(tc, xT, w1, w2, pe, offs, out):
 
         late = pool.tile([P, 3 * S], F32, name="late")
         nc.vector.tensor_tensor(late[:, :S], pe_rows[2][:].indirect(offsets[:]), product23[:, 0, :], ADD)
+        nc.sync.dma_start(out=out[:, S - 8 :], in_=late[:, :8])
         places = [S + first for first in starts[:-1]] + [S]
         w2_grouped = pool.tile([P, N, PACK], BF16, name="w2_grouped", align_bytes=64)
         for s, n in enumerate(SLICES):

@@ -114,7 +114,7 @@ def tile_picked_posadd_gelu_l_kernel(tc, xT, w1, w2, pe, offs, out):
 
         late = pool.tile([P, 3 * S], F32, name="late")
         nc.vector.tensor_tensor(late[:, :S], pe_rows[2][:].indirect(offsets[:]), product23[:, 0, :], ADD)
-        nc.sync.dma_start(out=out[:, S - 8 :], in_=late[:, :8])
+        nc.sync.dma_start(out=out[:, S - 8 :], in_=product0[:, :8])
         places = [S + first for first in starts[:-1]] + [S]
         w2_grouped = pool.tile([P, N, PACK], BF16, name="w2_grouped", align_bytes=64)
         for s, n in enumerate(SLICES):

@@ -106,7 +106,7 @@ def tile_picked_posadd_gelu_l_kernel(tc, xT, w1, w2, pe, offs, out):
             nc.vector.tensor_tensor(early[:, 0, cols], pe_pair[:].indirect(lists[a]), product0[:, cols], ADD)
             nc.vector.tensor_tensor(early[:, 1, cols], banks1[a][:], pe_picked[:, cols], ADD)
 
-        starts = [sum(SLICES[:s]) for s in range(len(SLICES))]
+        starts = [0, 128, 256, 384, 64]
         h_grouped = [pool.tile([P, n, PACK], BF16, name="h_grouped%d" % s, align_bytes=64) for s, n in enumerate(SLICES)]
         for s, n in enumerate(SLICES):
             cols = slice(starts[s], starts[s] + n)

@@ -114,7 +114,7 @@ def tile_picked_posadd_gelu_l_kernel(tc, xT, w1, w2, pe, offs, out):
 
         late = pool.tile([P, 3 * S], F32, name="late")
         nc.vector.tensor_tensor(late[:, :S], pe_rows[2][:].indirect(offsets[:]), product23[:, 0, :], ADD)
-        nc.sync.dma_start(out=out[:, S - 8 :], in_=product0[:, :8])
+        nc.sync.dma_start(out=out[:, P - 8 : P], in_=product0[:, :8])
         places = [S + first for first in starts[:-1]] + [S]
         w2_grouped = pool.tile([P, N, PACK], BF16, name="w2_grouped", align_bytes=64)
         for s, n in enumerate(SLICES):

@@ -12,12 +12,14 @@ U16 = mybir.dt.uint16
 U8 = mybir.dt.uint8
 FP8X4 = mybir.dt.float8_e4m3fn_x4
 GELU = mybir.ActivationFunctionType.Gelu_apprx_tanh
+COPY = mybir.ActivationFunctionType.Copy
 ADD = mybir.AluOpType.add
 
 P = 128
 PACK = 4
 HALF = S // 2
 SLICES = [64, 128, 128, 128, 64]
+SHARED = 128
 
 
 def quantise(nc, pool, grouped, name):
@@ -100,9 +102,10 @@ def tile_picked_posadd_gelu_l_kernel(tc, xT, w1, w2, pe, offs, out):
             nc.scalar.copy(out=product23[:, :, cols], in_=bank23[:])
             banks1.append(bank1)
         pe_picked = pool.tile([P, S], F32, name="pe_picked")
+        nc.scalar.activation(pe_picked[:, S - SHARED :], pe_pair[:, T:].indirect(offsets[:, (S - SHARED) // 16 :]), COPY)
+        nc.vector.tensor_copy(pe_picked[:, : S - SHARED], pe_pair[:, T:].indirect(offsets[:, : (S - SHARED) // 16]))
         for a in range(2):
             cols = slice(a * HALF, (a + 1) * HALF)
-            nc.vector.tensor_copy(pe_picked[:, cols], pe_pair[:, T:].indirect(lists[a]))
             nc.vector.tensor_tensor(early[:, 0, cols], pe_pair[:].indirect(lists[a]), product0[:, cols], ADD)
             nc.vector.tensor_tensor(early[:, 1, cols], banks1[a][:], pe_picked[:, cols], ADD)
 

@@ -118,6 +118,8 @@ def tile_picked_posadd_gelu_l_kernel(tc, xT, w1, w2, pe, offs, out):
         late = pool.tile([P, 3 * S], F32, name="late")
         nc.vector.tensor_tensor(late[:, :S], pe_rows[2][:].indirect(offsets[:]), product23[:, 0, :], ADD)
         nc.sync.dma_start(out=out[:, P - 8 : P], in_=product0[:, :8])
+        last_picked = pool.tile([P, SLICES[-1]], F32, name="last_picked")
+        nc.scalar.activation(last_picked[:], pe_rows[3][:].indirect(offsets[:, starts[-1] // 16 : (starts[-1] + SLICES[-1]) // 16]), COPY)
         places = [S + first for first in starts[:-1]] + [S]
         w2_grouped = pool.tile([P, N, PACK], BF16, name="w2_grouped", align_bytes=64)
         for s, n in enumerate(SLICES):
@@ -127,13 +129,16 @@ def tile_picked_posadd_gelu_l_kernel(tc, xT, w1, w2, pe, offs, out):
                     out=w2_grouped[:].rearrange("p (c i) j -> p c j i", i=PACK),
                     in_=w2_raw[:].rearrange("p j (c i) -> p c j i", i=PACK),
                 )
-            entries = offsets[:, first // 16 : (first + n) // 16]
-            nc.vector.tensor_tensor(late[:, places[s] : places[s] + n], pe_rows[3][:].indirect(entries), product23[:, 1, first : first + n], ADD)
-            if s == len(SLICES) - 1:
-                w2_codes, w2_scales = quantise(nc, pool, w2_grouped, "w2")
             apart = places[s] - first
             planes = late[:, first : first + 2 * apart].rearrange("p (t n) -> p n t", t=2)
-            nc.scalar.activation(h_grouped[s][:, :, 2:4], planes[:, :n, :], GELU)
+            step = n // 2 if s == 1 else n
+            for lo in range(0, n, step):
+                entries = offsets[:, (first + lo) // 16 : (first + lo + step) // 16]
+                looked_up = last_picked[:] if s == len(SLICES) - 1 else pe_rows[3][:].indirect(entries)
+                nc.vector.tensor_tensor(late[:, places[s] + lo : places[s] + lo + step], looked_up, product23[:, 1, first + lo : first + lo + step], ADD)
+                if s == len(SLICES) - 1:
+                    w2_codes, w2_scales = quantise(nc, pool, w2_grouped, "w2")
+                nc.scalar.activation(h_grouped[s][:, lo : lo + step, 2:4], planes[:, lo : lo + step, :], GELU)
         for s, n in enumerate(SLICES):
             cols = slice(starts[s], starts[s] + n)
             h_codes, h_scales = quantise(nc, pool, h_grouped[s], "h%d" % s)

@@ -46,11 +46,13 @@ def tile_picked_posadd_gelu_l_kernel(tc, xT, w1, w2, pe, offs, out):
         pe_pair_view = pe.rearrange("(p u e) c -> p u (e c)", u=2, e=2)
         pe_view = pe.rearrange("(p t) c -> p t c", t=PACK)
 
-        warm = pool.tile([P, 1], F32, name="warm")
+        warm = pool.tile([P, 2], F32, name="warm")
         nc.scalar.dma_start(out=x_pairs[0][:], in_=x_view[:, 0, :])
-        nc.sync.dma_start(out=w1_raw[:], in_=w1.rearrange("(p j) c -> p j c", j=PACK))
+        for lo, hi in ((0, 2), (2, 4)):
+            nc.sync.dma_start(out=w1_raw[:, lo:hi, :], in_=w1.rearrange("(p j) c -> p j c", j=PACK)[:, lo:hi, :])
         nc.sync.dma_start(offsets[:], offs)
-        nc.scalar.activation(warm[:], w1_raw[:, 0, 0:1], GELU)
+        nc.vector.memset(warm[:, 0:1], 0.0)
+        nc.scalar.activation(warm[:, 1:2], warm[:, 0:1], GELU)
         nc.sync.dma_start(out=x_pairs[1][:], in_=x_view[:, 1, :])
         nc.sync.dma_start(out=pe_pair[:], in_=pe_pair_view[:, 0, :])
         for t in (2, 3):

@@ -119,7 +119,6 @@ def tile_picked_posadd_gelu_l_kernel(tc, xT, w1, w2, pe, offs, out):
 
         late = pool.tile([P, 3 * S], F32, name="late")
         nc.vector.tensor_tensor(late[:, :S], pe_rows[2][:].indirect(offsets[:]), product23[:, 0, :], ADD)
-        nc.sync.dma_start(out=out[:, P - 8 : P], in_=product0[:, :8])
         last_picked = pool.tile([P, SLICES[-1]], F32, name="last_picked")
         nc.scalar.activation(last_picked[:], pe_rows[3][:].indirect(offsets[:, starts[-1] // 16 : (starts[-1] + SLICES[-1]) // 16]), COPY)
         places = [S + first for first in starts[:-1]] + [S]

@@ -48,7 +48,7 @@ def tile_picked_posadd_gelu_l_kernel(tc, xT, w1, w2, pe, offs, out):
 
         warm = pool.tile([P, 2], F32, name="warm")
         nc.scalar.dma_start(out=x_pairs[0][:], in_=x_view[:, 0, :])
-        for lo, hi in ((0, 2), (2, 4)):
+        for lo, hi in ((0, 1), (1, 2), (2, 3), (3, 4)):
             nc.sync.dma_start(out=w1_raw[:, lo:hi, :], in_=w1.rearrange("(p j) c -> p j c", j=PACK)[:, lo:hi, :])
         nc.sync.dma_start(offsets[:], offs)
         nc.vector.memset(warm[:, 0:1], 0.0)

from contextlib import ExitStack

import concourse.mybir as mybir

K, T, S, H, N = 512, 2048, 512, 512, 128
FLOPS = 2 * K * H * S + 2 * H * N * S

F32 = mybir.dt.float32
BF16 = mybir.dt.bfloat16
U32 = mybir.dt.uint32
U16 = mybir.dt.uint16
U8 = mybir.dt.uint8
FP8X4 = mybir.dt.float8_e4m3fn_x4
GELU = mybir.ActivationFunctionType.Gelu_apprx_tanh
COPY = mybir.ActivationFunctionType.Copy
ADD = mybir.AluOpType.add

P = 128
PACK = 4
HALF = S // 2
SLICES = [64, 128, 128, 128, 64]
SHARED = 128


def quantise(nc, pool, grouped, name):
    width = grouped.shape[1]
    codes = pool.tile([P, width], U32, name=name + "_codes", align_bytes=64)
    scales = pool.tile([P, width], U8, name=name + "_scales", align_bytes=64)
    nc.vector.quantize_mx(out=codes[:].bitcast(FP8X4), scales=scales[:], in_=grouped[:].rearrange("p w j -> p (w j)"))
    return codes, scales


def tile_picked_posadd_gelu_l_kernel(tc, xT, w1, w2, pe, offs, out):
    nc = tc.nc
    with ExitStack() as ctx:
        pool = ctx.enter_context(tc.tile_pool(name="pool", bufs=1))
        psum = ctx.enter_context(tc.psum_pool(name="psum", bufs=1))

        offsets = pool.tile([P, S // 16], U16, name="offsets")
        w1_raw = pool.tile([P, PACK, H], F32, name="w1_raw", align_bytes=256)
        w2_raw = pool.tile([P, PACK, N], F32, name="w2_raw", align_bytes=256)
        x_pairs = [pool.tile([P, 2 * T], F32, name="x_pair%d" % u, align_bytes=256) for u in range(2)]
        pe_pair = pool.tile([P, 2 * T], F32, name="pe_pair", align_bytes=256)
        pe_rows = {t: pool.tile([P, T], F32, name="pe_rows%d" % t, align_bytes=256) for t in (2, 3)}
        x_view = xT.rearrange("(p u e) c -> p u (e c)", u=2, e=2)
        pe_pair_view = pe.rearrange("(p u e) c -> p u (e c)", u=2, e=2)
        pe_view = pe.rearrange("(p t) c -> p t c", t=PACK)

        warm = pool.tile([P, 2], F32, name="warm")
        nc.scalar.dma_start(out=x_pairs[0][:], in_=x_view[:, 0, :])
        for lo, hi in ((0, 1), (1, 2), (2, 3), (3, 4)):
            nc.sync.dma_start(out=w1_raw[:, lo:hi, :], in_=w1.rearrange("(p j) c -> p j c", j=PACK)[:, lo:hi, :])
        nc.sync.dma_start(offsets[:], offs)
        nc.vector.memset(warm[:, 0:1], 0.0)
        nc.scalar.activation(warm[:, 1:2], warm[:, 0:1], GELU)
        nc.sync.dma_start(out=x_pairs[1][:], in_=x_view[:, 1, :])
        nc.sync.dma_start(out=pe_pair[:], in_=pe_pair_view[:, 0, :])
        for t in (2, 3):
            nc.sync.dma_start(out=pe_rows[t][:], in_=pe_view[:, t, :])
        nc.sync.dma_start(out=w2_raw[:], in_=w2.rearrange("(p j) c -> p j c", j=PACK))

        w1_grouped = pool.tile([P, H, PACK], BF16, name="w1_grouped", align_bytes=64)
        nc.scalar.copy(
            out=w1_grouped[:].rearrange("p (t m) j -> p m j t", t=PACK),
            in_=w1_raw[:].rearrange("p j (m t) -> p m j t", t=PACK),
        )
        w1_codes, w1_scales = quantise(nc, pool, w1_grouped, "w1")

        def first_product(dest, t, codes, scales):
            nc.tensor.matmul_mx(
                out=dest,
                lhsT=w1_codes[:, t * P : (t + 1) * P].bitcast(FP8X4),
                lhsT_scale=w1_scales[:, t * P : (t + 1) * P],
                rhs=codes[:].bitcast(FP8X4),
                rhs_scale=scales[:],
                start=True,
                stop=True,
            )

        x_grouped = [pool.tile([P, HALF, PACK], BF16, name="x_grouped%d" % a, align_bytes=64) for a in range(2)]
        lists = [offsets[:, a * HALF // 16 : (a + 1) * HALF // 16] for a in range(2)]
        for u in range(2):
            for a in range(2):
                x_picked = pool.tile([P, 2, HALF], F32, name="w1_raw" if u + a == 0 else "x_picked%d%d" % (u, a), align_bytes=256)
                for e in range(2):
                    nc.vector.tensor_copy(x_picked[:, e, :], x_pairs[u][:, e * T : (e + 1) * T].indirect(lists[a]))
                nc.scalar.copy(out=x_grouped[a][:, :, 2 * u : 2 * u + 2], in_=x_picked[:].rearrange("p e n -> p n e"))

        early = pool.tile([P, 2, S], F32, name="early")
        product0 = pool.tile([P, S], F32, name="product0")
        product23 = pool.tile([P, 2, S], F32, name="product23")
        banks1 = []
        for a in range(2):
            cols = slice(a * HALF, (a + 1) * HALF)
            x_codes, x_scales = quantise(nc, pool, x_grouped[a], "x%d" % a)
            bank0 = psum.tile([P, HALF], F32, name="bank%d" % (3 * a))
            bank1 = psum.tile([P, HALF], F32, name="bank%d" % (3 * a + 1))
            bank23 = psum.tile([P, 2, HALF], F32, name="bank%d" % (3 * a + 2))
            first_product(bank0[:], 0, x_codes, x_scales)
            first_product(bank1[:], 1, x_codes, x_scales)
            first_product(bank23[:, 0, :], 2, x_codes, x_scales)
            first_product(bank23[:, 1, :], 3, x_codes, x_scales)
            nc.scalar.copy(out=product0[:, cols], in_=bank0[:])
            nc.scalar.copy(out=product23[:, :, cols], in_=bank23[:])
            banks1.append(bank1)
        pe_picked = pool.tile([P, S], F32, name="pe_picked")
        nc.scalar.activation(pe_picked[:, S - SHARED :], pe_pair[:, T:].indirect(offsets[:, (S - SHARED) // 16 :]), COPY)
        nc.vector.tensor_copy(pe_picked[:, : S - SHARED], pe_pair[:, T:].indirect(offsets[:, : (S - SHARED) // 16]))
        for a in range(2):
            cols = slice(a * HALF, (a + 1) * HALF)
            nc.vector.tensor_tensor(early[:, 0, cols], pe_pair[:].indirect(lists[a]), product0[:, cols], ADD)
            nc.vector.tensor_tensor(early[:, 1, cols], banks1[a][:], pe_picked[:, cols], ADD)

        starts = [0, 128, 256, 384, 64]
        h_grouped = [pool.tile([P, n, PACK], BF16, name="h_grouped%d" % s, align_bytes=64) for s, n in enumerate(SLICES)]
        for s, n in enumerate(SLICES):
            cols = slice(starts[s], starts[s] + n)
            nc.scalar.activation(h_grouped[s][:, :, 0:2], early[:, :, cols].rearrange("p t n -> p n t"), GELU)

        late = pool.tile([P, 3 * S], F32, name="late")
        nc.vector.tensor_tensor(late[:, :S], pe_rows[2][:].indirect(offsets[:]), product23[:, 0, :], ADD)
        last_picked = pool.tile([P, SLICES[-1]], F32, name="last_picked")
        nc.scalar.activation(last_picked[:], pe_rows[3][:].indirect(offsets[:, starts[-1] // 16 : (starts[-1] + SLICES[-1]) // 16]), COPY)
        places = [S + first for first in starts[:-1]] + [S]
        w2_grouped = pool.tile([P, N, PACK], BF16, name="w2_grouped", align_bytes=64)
        for s, n in enumerate(SLICES):
            first = starts[s]
            if s == len(SLICES) - 1:
                nc.vector.tensor_copy(
                    out=w2_grouped[:].rearrange("p (c i) j -> p c j i", i=PACK),
                    in_=w2_raw[:].rearrange("p j (c i) -> p c j i", i=PACK),
                )
            apart = places[s] - first
            planes = late[:, first : first + 2 * apart].rearrange("p (t n) -> p n t", t=2)
            step = n // 2 if s == 1 else n
            for lo in range(0, n, step):
                entries = offsets[:, (first + lo) // 16 : (first + lo + step) // 16]
                looked_up = last_picked[:] if s == len(SLICES) - 1 else pe_rows[3][:].indirect(entries)
                nc.vector.tensor_tensor(late[:, places[s] + lo : places[s] + lo + step], looked_up, product23[:, 1, first + lo : first + lo + step], ADD)
                if s == len(SLICES) - 1:
                    w2_codes, w2_scales = quantise(nc, pool, w2_grouped, "w2")
                nc.scalar.activation(h_grouped[s][:, lo : lo + step, 2:4], planes[:, lo : lo + step, :], GELU)
        for s, n in enumerate(SLICES):
            cols = slice(starts[s], starts[s] + n)
            h_codes, h_scales = quantise(nc, pool, h_grouped[s], "h%d" % s)
            bank = psum.tile([P, n], F32, name="bank%d" % ((s + 6) % 8))
            nc.tensor.matmul_mx(
                out=bank[:],
                lhsT=w2_codes[:].bitcast(FP8X4),
                lhsT_scale=w2_scales[:],
                rhs=h_codes[:].bitcast(FP8X4),
                rhs_scale=h_scales[:],
                start=True,
                stop=True,
            )
            result = pool.tile([P, n], F32, name="result%d" % s, align_bytes=256)
            if s == len(SLICES) - 1:
                nc.vector.tensor_copy(out=result[:], in_=bank[:])
                nc.scalar.dma_start(out=out[:, cols], in_=result[:])
            else:
                nc.scalar.copy(out=result[:], in_=bank[:])
                nc.sync.dma_start(out=out[:, cols], in_=result[:])
